import numpy as np, ml_dtypes
CORES = [5,21,45,77,85,101,109,125,133,141,189,213]
N = 12
import mx_ref
KT = 1
BF = ml_dtypes.bfloat16
def setup_inputs(rng):
    def f(*shape):
        return mx_ref.flush((rng.standard_normal(shape, dtype=np.float32) * np.exp2(rng.integers(-2, 3, shape[:-1] + (1,)))).astype(BF))
    return {"x": f(N, 128, KT * 512)}
def setup_inputs_blocks(rng):
    d = setup_inputs(rng)
    for k in ("x",): d[k] = mx_ref.spread(d[k], rng, 4)
    return d
def setup_inputs_wide(rng):
    d = setup_inputs(rng)
    for k in ("x",): d[k] = mx_ref.flush((d[k].astype(np.float32) * np.exp2(rng.integers(-8, 9, (N, 1, 1))).astype(np.float32)).astype(BF))
    return d
def setup_inputs_zeros(rng):
    d = setup_inputs(rng); v = d["x"].reshape(N, 128, -1, 4).copy()
    v[np.broadcast_to((rng.random((N, 1, v.shape[2], 1)) < 0.33), v.shape)] = 0
    d["x"] = v.reshape(d["x"].shape)
    return d
def reference(x):
    Q = [[mx_ref.quantize(x[j][:, 512 * t:512 * t + 512]) for t in range(KT)] for j in range(N)]
    y = np.zeros((N, 128, N * 128), np.float32)
    for r in range(N):
        for j in range(N):
            for t in range(KT):
                p = mx_ref.matmul(Q[r][t], Q[j][t])
                y[r][:, 128 * j:128 * j + 128] = p if t == 0 else y[r][:, 128 * j:128 * j + 128] + p
    return {"y": y}

from concourse.bass import DstId, RemoteDMATransfer
from concourse.mybir import dt

N = 12
W = 128
BANK = 512
BANKS = 8

SCRATCH = {
    "xin": ("sbuf", [128, 4 * W], "bfloat16"),
    "q": ("sbuf", [128, N * W], "float8_e4m3fn_x4"),
    "s": ("sbuf", [128, N * W], "uint8"),
    "res": ("sbuf", [128, N * W], "float32"),
    "acc": ("psum", [128, BANKS * BANK], "float32"),
}
SEMAPHORES = (["ld", "qz", "fs", "fc", "sent", "st0", "st1"]
              + ["t%d" % j for j in range(N)] + ["mm%d" % j for j in range(N)] + ["cp%d" % j for j in range(N)])

SHARES = (
    ("far", 0, (("x", 0), ("s", 1), ("x", 1))),
    ("far", 1, (("s", 2), ("x", 2))),
    ("near", 0, (("x", 3), ("x", 4))),
    ("near", 1, (("s", 3), ("x", 5))),
)
DIRECT = (("s", 4), ("s", 5))


def _on_chip(topo, a, b):
    return topo.host(a) == topo.host(b) and topo.chip(a) == topo.chip(b)


def _plan(T, topo, r):
    cores = T.cores
    c = cores[r]
    own = [k for k in range(N) if k == r or topo.same_plane(c, cores[k])]
    oth = [k for k in range(N) if k not in own]
    i = own.index(r)

    def who(kind, k):
        return own[(i + k) % len(own)] if kind == "s" else oth[(i + k) % len(oth)]

    span = range(topo.host(c) * topo.CORES_PER_HOST, (topo.host(c) + 1) * topo.CORES_PER_HOST)
    owners = [d for d in span if d != c and _on_chip(topo, c, d) and topo.may_write(d, cores[oth[0]])]
    side = {"near": [d for d in owners if topo.die(d) == topo.die(c)],
            "far": [d for d in owners if topo.die(d) != topo.die(c)]}
    plan = [(side[where][n], [who(*e) for e in share]) for where, n, share in SHARES]
    plan.append((c, [who(*e) for e in DIRECT]))
    return plan


def _mask(topo, src, dsts):
    m = topo.mask(src, dsts[0])
    for d in dsts[1:]:
        m &= topo.mask(src, d)
    return m


def _engines(m):
    return bin(m).count("1")


def _send(g, T, topo, core, j, dsts, codes, sem):
    def view():
        return T.q[:, j * W:(j + 1) * W].bitcast(dt.uint8) if codes else T.s[:, j * W:(j + 1) * W]
    ids = []
    for d in dsts:
        rid, pid = topo.addr(d, core)
        ids.append(DstId(rid=rid, pnc=pid))
    m = _mask(topo, core, dsts)
    g.remote_dma_fused([RemoteDMATransfer(dst_ids=ids, dma_engine_mask=m, remote_sem=sem,
                                          srcs=[view()], dsts=[view() for _ in dsts])], local_sem=T.sem.sent)
    return _engines(m)


def _relay(g, T, topo, core, j, feeder, fed, ranks):
    n = _engines(_mask(topo, feeder, fed))
    dsts = [T.cores[k] for k in ranks]
    g.wait_ge(T.sem.fs, n)
    left = _send(g, T, topo, core, j, dsts, False, T.sem["t%d" % j])
    g.wait_ge(T.sem.fc, n)
    left += _send(g, T, topo, core, j, dsts, True, T.sem["t%d" % j])
    g.wait_ge(T.sem.sent, left)


def rank_program(g, core, T, topo):
    rank = T.rank_of(core)
    if rank is None:
        for j in range(N):
            if _on_chip(topo, core, T.cores[j]):
                plan = _plan(T, topo, j)
                fed = [c for c, _ in plan[:-1]]
                for c, ranks in plan[:-1]:
                    if c == core:
                        _relay(g, T, topo, core, j, T.cores[j], fed, ranks)
        return

    def blk(j):
        return slice(j * W, (j + 1) * W)

    g.sync.dma_start(T.xin[:], T.x[:]).then_inc(T.sem.ld, 16)
    g.vector.wait_ge(T.sem.ld, 16)
    g.vector.quantize_mx(T.q[:, blk(rank)], T.s[:, blk(rank)], T.xin[:]).then_inc(T.sem.qz, 1)

    plan = _plan(T, topo, rank)
    fed = [c for c, _ in plan[:-1]]
    direct = [T.cores[k] for k in plan[-1][1]]
    g.wait_ge(T.sem.qz, 1)
    left = _send(g, T, topo, core, rank, fed, False, T.sem.fs)
    left += _send(g, T, topo, core, rank, fed, True, T.sem.fc)
    left += _send(g, T, topo, core, rank, direct, False, T.sem["t%d" % rank])
    left += _send(g, T, topo, core, rank, direct, True, T.sem["t%d" % rank])

    due = []
    for j in range(N):
        if j == rank:
            continue
        pj = _plan(T, topo, j)
        for n, (c, ranks) in enumerate(pj):
            if rank in ranks:
                turn = ranks.index(rank)
                place = -1 if c == T.cores[j] else n
                due.append((turn, place, j, 2 * _engines(_mask(topo, c, [T.cores[k] for k in ranks]))))
    due.sort()
    order = [(rank, 0)] + [(j, n) for _, _, j, n in due]

    stores = [0, 0]
    g.tensor.wait_ge(T.sem.qz, 1)
    for k, (j, n) in enumerate(order):
        bank = T.acc[:, (k % BANKS) * BANK:(k % BANKS) * BANK + W]
        if n:
            g.tensor.wait_ge(T.sem["t%d" % j], n)
        if k >= BANKS:
            g.tensor.wait_ge(T.sem["cp%d" % order[k - BANKS][0]], 1)
        g.tensor.matmul_mx(bank, T.q[:, blk(rank)], T.s[:, blk(rank)], T.q[:, blk(j)], T.s[:, blk(j)],
                           True, True).then_inc(T.sem["mm%d" % j], 1)
        g.vector.wait_ge(T.sem["mm%d" % j], 1)
        g.vector.tensor_copy(T.res[:, blk(j)], bank).then_inc(T.sem["cp%d" % j], 1)
        queue = (g.sync, g.scalar)[k % 2]
        queue.wait_ge(T.sem["cp%d" % j], 1)
        queue.dma_start(T.y[:, blk(j)], T.res[:, blk(j)]).then_inc(T.sem["st%d" % (k % 2)], 16)
        stores[k % 2] += 16
    g.sync.wait_ge(T.sem.st0, stores[0])
    g.scalar.wait_ge(T.sem.st1, stores[1])
    g.wait_ge(T.sem.sent, left)
